import numpy as np
import ml_dtypes

BF16 = ml_dtypes.bfloat16


def bf(x):
    return np.asarray(x, np.float32).astype(BF16)


def f32(x):
    return np.asarray(x, np.float32)


def f64(x):
    return np.asarray(x).astype(np.float64)


def striped(idx):
    return np.tile(idx.reshape(-1, 16).T, (8, 1))


S, K, M, N, D, V = 512, 256, 256, 1024, 4, 256


def setup_inputs():
    return {"table": bf(np.random.standard_normal((K, S))), "w": bf(np.random.standard_normal((K, M)) / np.sqrt(K)), "b": f32(0.5 * np.random.standard_normal((M, 1))), "offs": striped(np.random.permutation(np.tile(np.arange(S), 2))[:N])}


def reference(table, w, b, offs):
    idx = offs[:16].T.reshape(-1)
    x = f64(table)[:, idx]
    y = f64(w).T @ x
    z = np.maximum(y + f64(b), 0.0)
    return z.reshape(M, V, D).max(axis=2)

@@ -1,0 +1,62 @@
+import concourse.mybir as mybir
+
+BF16, F32, U16 = mybir.dt.bfloat16, mybir.dt.float32, mybir.dt.uint16
+ADD, MAX = mybir.AluOpType.add, mybir.AluOpType.max
+
+P = 128
+K, S = 256, 512
+M = 256
+N, D = 1024, 4
+PIECE = 256
+K_BLOCKS = K // P
+M_BLOCKS = M // P
+PIECES = N // PIECE
+PIECE_COLS = PIECE // 16
+PIECE_NODES = PIECE // D
+
+FLOPS = 2 * K * M * N
+
+
+def tile_gather_matmul_kernel(tc, table, w, b, offs, out):
+    nc = tc.nc
+    with (
+        tc.tile_pool(name="held", bufs=1) as held,
+        tc.psum_pool(name="products", bufs=M_BLOCKS * PIECES) as products,
+    ):
+        offsets = held.tile([P, N // 16], U16, name="offsets")
+        nc.sync.dma_start(offsets[:], offs)
+
+        weights = held.tile([P, K_BLOCKS, M], BF16, name="weights")
+        nc.scalar.dma_start(weights[:], w.rearrange("(kb p) m -> p kb m", p=P))
+
+        windows = []
+        for kb, queue in zip(range(K_BLOCKS), (nc.sync, nc.scalar)):
+            window = held.tile([P, S], BF16, name="window%d" % kb)
+            queue.dma_start(window[:], table[kb * P : (kb + 1) * P, :])
+            windows.append(window)
+
+        bias = held.tile([P, M_BLOCKS], F32, name="bias")
+        nc.gpsimd.dma_start(bias[:], b.rearrange("(mb p) o -> p (mb o)", p=P))
+
+        for mb in range(M_BLOCKS):
+            pooled = held.tile([P, N // D], F32, name="pooled%d" % mb)
+            for q in range(PIECES):
+                piece = offsets[:, q * PIECE_COLS : (q + 1) * PIECE_COLS]
+                y = products.tile([P, PIECE], F32, name="y")
+                for kb in range(K_BLOCKS):
+                    nc.tensor.matmul(
+                        y[:],
+                        weights[:, kb, mb * P : (mb + 1) * P],
+                        windows[kb][:].indirect(piece),
+                        start=(kb == 0),
+                        stop=(kb == K_BLOCKS - 1),
+                    )
+                nc.vector.tensor_reduce(
+                    pooled[:, q * PIECE_NODES : (q + 1) * PIECE_NODES],
+                    y[:].rearrange("p (v d) -> p v d", d=D),
+                    axis=mybir.AxisListType.X,
+                    op=MAX,
+                )
+            result = held.tile([P, N // D], F32, name="result%d" % mb)
+            nc.vector.tensor_scalar(result[:], pooled[:], bias[:, mb : mb + 1], 0.0, op0=ADD, op1=MAX)
+            nc.sync.dma_start(out[mb * P : (mb + 1) * P, :], result[:])

@@ -13,6 +13,7 @@ M_BLOCKS = M // P
 PIECES = N // PIECE
 PIECE_COLS = PIECE // 16
 PIECE_NODES = PIECE // D
+WARM_UPS = 14
 
 FLOPS = 2 * K * M * N
 
@@ -21,7 +22,8 @@ def tile_gather_matmul_kernel(tc, table, w, b, offs, out):
     nc = tc.nc
     with (
         tc.tile_pool(name="held", bufs=1) as held,
-        tc.psum_pool(name="products", bufs=M_BLOCKS * PIECES) as products,
+        tc.psum_pool(name="products", bufs=PIECES) as products,
+        tc.psum_pool(name="scratch", bufs=1) as scratch,
     ):
         offsets = held.tile([P, N // 16], U16, name="offsets")
         nc.sync.dma_start(offsets[:], offs)
@@ -36,7 +38,13 @@ def tile_gather_matmul_kernel(tc, table, w, b, offs, out):
             windows.append(window)
 
         bias = held.tile([P, M_BLOCKS], F32, name="bias")
-        nc.gpsimd.dma_start(bias[:], b.rearrange("(mb p) o -> p (mb o)", p=P))
+        nc.scalar.dma_start(bias[:], b.rearrange("(mb p) o -> p (mb o)", p=P))
+
+        zeros = held.tile([P, P], BF16, name="zeros")
+        nc.vector.memset(zeros[:], 0.0)
+        unread = scratch.tile([P, P], F32, name="unread")
+        for i in range(WARM_UPS):
+            nc.tensor.matmul(unread[:], zeros[:], zeros[:], start=True, stop=True)
 
         for mb in range(M_BLOCKS):
             pooled = held.tile([P, N // D], F32, name="pooled%d" % mb)

@@ -22,6 +22,7 @@ def tile_gather_matmul_kernel(tc, table, w, b, offs, out):
     nc = tc.nc
     with (
         tc.tile_pool(name="held", bufs=1) as held,
+        tc.tile_pool(name="ring", bufs=2) as ring,
         tc.psum_pool(name="products", bufs=PIECES) as products,
         tc.psum_pool(name="scratch", bufs=1) as scratch,
     ):
@@ -47,8 +48,9 @@ def tile_gather_matmul_kernel(tc, table, w, b, offs, out):
             nc.tensor.matmul(unread[:], zeros[:], zeros[:], start=True, stop=True)
 
         for mb in range(M_BLOCKS):
-            pooled = held.tile([P, N // D], F32, name="pooled%d" % mb)
+            result = held.tile([P, N // D], F32, name="result%d" % mb)
             for q in range(PIECES):
+                nodes = slice(q * PIECE_NODES, (q + 1) * PIECE_NODES)
                 piece = offsets[:, q * PIECE_COLS : (q + 1) * PIECE_COLS]
                 y = products.tile([P, PIECE], F32, name="y")
                 for kb in range(K_BLOCKS):
@@ -59,12 +61,12 @@ def tile_gather_matmul_kernel(tc, table, w, b, offs, out):
                         start=(kb == 0),
                         stop=(kb == K_BLOCKS - 1),
                     )
+                pooled = ring.tile([P, PIECE_NODES], F32, name="pooled")
                 nc.vector.tensor_reduce(
-                    pooled[:, q * PIECE_NODES : (q + 1) * PIECE_NODES],
+                    pooled[:],
                     y[:].rearrange("p (v d) -> p v d", d=D),
                     axis=mybir.AxisListType.X,
                     op=MAX,
                 )
-            result = held.tile([P, N // D], F32, name="result%d" % mb)
-            nc.vector.tensor_scalar(result[:], pooled[:], bias[:, mb : mb + 1], 0.0, op0=ADD, op1=MAX)
-            nc.sync.dma_start(out[mb * P : (mb + 1) * P, :], result[:])
+                nc.vector.tensor_scalar(result[:, nodes], pooled[:], bias[:, mb : mb + 1], 0.0, op0=ADD, op1=MAX)
+                nc.sync.dma_start(out[mb * P : (mb + 1) * P, nodes], result[:, nodes])

@@ -47,26 +47,39 @@ def tile_gather_matmul_kernel(tc, table, w, b, offs, out):
         for i in range(WARM_UPS):
             nc.tensor.matmul(unread[:], zeros[:], zeros[:], start=True, stop=True)
 
+        def look_up(y, mb, q, kb):
+            nc.tensor.matmul(
+                y[:],
+                weights[:, kb, mb * P : (mb + 1) * P],
+                windows[kb][:].indirect(offsets[:, q * PIECE_COLS : (q + 1) * PIECE_COLS]),
+                start=(kb == 0),
+                stop=(kb == K_BLOCKS - 1),
+            )
+
+        def finish(y, mb, q):
+            nodes = slice(q * PIECE_NODES, (q + 1) * PIECE_NODES)
+            pooled = ring.tile([P, PIECE_NODES], F32, name="pooled")
+            nc.vector.tensor_reduce(
+                pooled[:],
+                y[:].rearrange("p (v d) -> p v d", d=D),
+                axis=mybir.AxisListType.X,
+                op=MAX,
+            )
+            nc.vector.tensor_scalar(results[mb][:, nodes], pooled[:], bias[:, mb : mb + 1], 0.0, op0=ADD, op1=MAX)
+            nc.sync.dma_start(out[mb * P : (mb + 1) * P, nodes], results[mb][:, nodes])
+
+        results = [held.tile([P, N // D], F32, name="result%d" % mb) for mb in range(M_BLOCKS)]
+
+        head = [products.tile([P, PIECE], F32, name="y") for q in range(2)]
+        for kb in range(K_BLOCKS):
+            for q in range(2):
+                look_up(head[q], 0, q, kb)
+        for q in range(2):
+            finish(head[q], 0, q)
+
         for mb in range(M_BLOCKS):
-            result = held.tile([P, N // D], F32, name="result%d" % mb)
-            for q in range(PIECES):
-                nodes = slice(q * PIECE_NODES, (q + 1) * PIECE_NODES)
-                piece = offsets[:, q * PIECE_COLS : (q + 1) * PIECE_COLS]
+            for q in range(2 if mb == 0 else 0, PIECES):
                 y = products.tile([P, PIECE], F32, name="y")
                 for kb in range(K_BLOCKS):
-                    nc.tensor.matmul(
-                        y[:],
-                        weights[:, kb, mb * P : (mb + 1) * P],
-                        windows[kb][:].indirect(piece),
-                        start=(kb == 0),
-                        stop=(kb == K_BLOCKS - 1),
-                    )
-                pooled = ring.tile([P, PIECE_NODES], F32, name="pooled")
-                nc.vector.tensor_reduce(
-                    pooled[:],
-                    y[:].rearrange("p (v d) -> p v d", d=D),
-                    axis=mybir.AxisListType.X,
-                    op=MAX,
-                )
-                nc.vector.tensor_scalar(result[:, nodes], pooled[:], bias[:, mb : mb + 1], 0.0, op0=ADD, op1=MAX)
-                nc.sync.dma_start(out[mb * P : (mb + 1) * P, nodes], result[:, nodes])
+                    look_up(y, mb, q, kb)
+                finish(y, mb, q)

@@ -13,7 +13,6 @@ M_BLOCKS = M // P
 PIECES = N // PIECE
 PIECE_COLS = PIECE // 16
 PIECE_NODES = PIECE // D
-WARM_UPS = 14
 
 FLOPS = 2 * K * M * N
 
@@ -24,33 +23,23 @@ def tile_gather_matmul_kernel(tc, table, w, b, offs, out):
         tc.tile_pool(name="held", bufs=1) as held,
         tc.tile_pool(name="ring", bufs=2) as ring,
         tc.psum_pool(name="products", bufs=PIECES) as products,
-        tc.psum_pool(name="scratch", bufs=1) as scratch,
     ):
         offsets = held.tile([P, N // 16], U16, name="offsets")
-        nc.sync.dma_start(offsets[:], offs)
-
-        weights = held.tile([P, K_BLOCKS, M], BF16, name="weights")
-        nc.scalar.dma_start(weights[:], w.rearrange("(kb p) m -> p kb m", p=P))
-
-        windows = []
-        for kb, queue in zip(range(K_BLOCKS), (nc.sync, nc.scalar)):
-            window = held.tile([P, S], BF16, name="window%d" % kb)
-            queue.dma_start(window[:], table[kb * P : (kb + 1) * P, :])
-            windows.append(window)
-
+        windows = [held.tile([P, S], BF16, name="window%d" % kb) for kb in range(K_BLOCKS)]
+        weights = [held.tile([P, K_BLOCKS, P], BF16, name="weights%d" % mb) for mb in range(M_BLOCKS)]
         bias = held.tile([P, M_BLOCKS], F32, name="bias")
-        nc.scalar.dma_start(bias[:], b.rearrange("(mb p) o -> p (mb o)", p=P))
 
-        zeros = held.tile([P, P], BF16, name="zeros")
-        nc.vector.memset(zeros[:], 0.0)
-        unread = scratch.tile([P, P], F32, name="unread")
-        for i in range(WARM_UPS):
-            nc.tensor.matmul(unread[:], zeros[:], zeros[:], start=True, stop=True)
+        nc.sync.dma_start(offsets[:], offs)
+        nc.scalar.dma_start(windows[0][:], table[0:P, :])
+        nc.sync.dma_start(weights[0][:], w[:, 0:P].rearrange("(kb p) m -> p kb m", p=P))
+        nc.scalar.dma_start(windows[1][:], table[P : 2 * P, :])
+        nc.sync.dma_start(bias[:], b.rearrange("(mb p) o -> p (mb o)", p=P))
+        nc.sync.dma_start(weights[1][:], w[:, P : 2 * P].rearrange("(kb p) m -> p kb m", p=P))
 
         def look_up(y, mb, q, kb):
             nc.tensor.matmul(
                 y[:],
-                weights[:, kb, mb * P : (mb + 1) * P],
+                weights[mb][:, kb, :],
                 windows[kb][:].indirect(offsets[:, q * PIECE_COLS : (q + 1) * PIECE_COLS]),
                 start=(kb == 0),
                 stop=(kb == K_BLOCKS - 1),

@@ -26,20 +26,27 @@ def tile_gather_matmul_kernel(tc, table, w, b, offs, out):
     ):
         offsets = held.tile([P, N // 16], U16, name="offsets")
         windows = [held.tile([P, S], BF16, name="window%d" % kb) for kb in range(K_BLOCKS)]
-        weights = [held.tile([P, K_BLOCKS, P], BF16, name="weights%d" % mb) for mb in range(M_BLOCKS)]
+        weights = [
+            [held.tile([P, P], BF16, name="weights%d_%d" % (mb, kb)) for kb in range(K_BLOCKS)] for mb in range(M_BLOCKS)
+        ]
         bias = held.tile([P, M_BLOCKS], F32, name="bias")
+
+        def load_weights(queue, mb, kb):
+            queue.dma_start(weights[mb][kb][:], w[kb * P : (kb + 1) * P, mb * P : (mb + 1) * P])
 
         nc.sync.dma_start(offsets[:], offs)
         nc.scalar.dma_start(windows[0][:], table[0:P, :])
-        nc.sync.dma_start(weights[0][:], w[:, 0:P].rearrange("(kb p) m -> p kb m", p=P))
+        load_weights(nc.sync, 0, 0)
         nc.scalar.dma_start(windows[1][:], table[P : 2 * P, :])
+        load_weights(nc.sync, 0, 1)
         nc.sync.dma_start(bias[:], b.rearrange("(mb p) o -> p (mb o)", p=P))
-        nc.sync.dma_start(weights[1][:], w[:, P : 2 * P].rearrange("(kb p) m -> p kb m", p=P))
+        load_weights(nc.scalar, 1, 0)
+        load_weights(nc.scalar, 1, 1)
 
         def look_up(y, mb, q, kb):
             nc.tensor.matmul(
                 y[:],
-                weights[mb][:, kb, :],
+                weights[mb][kb][:],
                 windows[kb][:].indirect(offsets[:, q * PIECE_COLS : (q + 1) * PIECE_COLS]),
                 start=(kb == 0),
                 stop=(kb == K_BLOCKS - 1),

@@ -37,10 +37,10 @@ def tile_gather_matmul_kernel(tc, table, w, b, offs, out):
         nc.sync.dma_start(offsets[:], offs)
         nc.scalar.dma_start(windows[0][:], table[0:P, :])
         load_weights(nc.sync, 0, 0)
-        nc.scalar.dma_start(windows[1][:], table[P : 2 * P, :])
-        load_weights(nc.sync, 0, 1)
-        nc.sync.dma_start(bias[:], b.rearrange("(mb p) o -> p (mb o)", p=P))
-        load_weights(nc.scalar, 1, 0)
+        load_weights(nc.scalar, 0, 1)
+        nc.sync.dma_start(windows[1][:], table[P : 2 * P, :])
+        nc.scalar.dma_start(bias[:], b.rearrange("(mb p) o -> p (mb o)", p=P))
+        load_weights(nc.sync, 1, 0)
         load_weights(nc.scalar, 1, 1)
 
         def look_up(y, mb, q, kb):
@@ -66,16 +66,15 @@ def tile_gather_matmul_kernel(tc, table, w, b, offs, out):
 
         results = [held.tile([P, N // D], F32, name="result%d" % mb) for mb in range(M_BLOCKS)]
 
-        head = [products.tile([P, PIECE], F32, name="y") for q in range(2)]
+        first_sums = [products.tile([P, PIECE], F32, name="y") for q in range(PIECES)]
         for kb in range(K_BLOCKS):
-            for q in range(2):
-                look_up(head[q], 0, q, kb)
-        for q in range(2):
-            finish(head[q], 0, q)
+            for q in range(PIECES):
+                look_up(first_sums[q], 0, q, kb)
+        for q in range(PIECES):
+            finish(first_sums[q], 0, q)
 
-        for mb in range(M_BLOCKS):
-            for q in range(2 if mb == 0 else 0, PIECES):
-                y = products.tile([P, PIECE], F32, name="y")
-                for kb in range(K_BLOCKS):
-                    look_up(y, mb, q, kb)
-                finish(y, mb, q)
+        for q in range(PIECES):
+            y = products.tile([P, PIECE], F32, name="y")
+            for kb in range(K_BLOCKS):
+                look_up(y, 1, q, kb)
+            finish(y, 1, q)

@@ -52,29 +52,34 @@ def tile_gather_matmul_kernel(tc, table, w, b, offs, out):
                 stop=(kb == K_BLOCKS - 1),
             )
 
-        def finish(y, mb, q):
-            nodes = slice(q * PIECE_NODES, (q + 1) * PIECE_NODES)
-            pooled = ring.tile([P, PIECE_NODES], F32, name="pooled")
-            nc.vector.tensor_reduce(
-                pooled[:],
-                y[:].rearrange("p (v d) -> p v d", d=D),
-                axis=mybir.AxisListType.X,
-                op=MAX,
-            )
-            nc.vector.tensor_scalar(results[mb][:, nodes], pooled[:], bias[:, mb : mb + 1], 0.0, op0=ADD, op1=MAX)
+        def pool_piece(pooled, y):
+            nc.vector.tensor_reduce(pooled, y[:].rearrange("p (v d) -> p v d", d=D), axis=mybir.AxisListType.X, op=MAX)
+
+        def bias_and_relu(mb, nodes, pooled):
+            nc.vector.tensor_scalar(results[mb][:, nodes], pooled, bias[:, mb : mb + 1], 0.0, op0=ADD, op1=MAX)
+
+        def store(mb, nodes):
             nc.sync.dma_start(out[mb * P : (mb + 1) * P, nodes], results[mb][:, nodes])
 
+        piece_nodes = [slice(q * PIECE_NODES, (q + 1) * PIECE_NODES) for q in range(PIECES)]
         results = [held.tile([P, N // D], F32, name="result%d" % mb) for mb in range(M_BLOCKS)]
 
         first_sums = [products.tile([P, PIECE], F32, name="y") for q in range(PIECES)]
         for kb in range(K_BLOCKS):
             for q in range(PIECES):
                 look_up(first_sums[q], 0, q, kb)
+        pooled_block = held.tile([P, N // D], F32, name="pooled_block")
         for q in range(PIECES):
-            finish(first_sums[q], 0, q)
+            pool_piece(pooled_block[:, piece_nodes[q]], first_sums[q])
+        bias_and_relu(0, slice(0, N // D), pooled_block[:])
+        for q in range(PIECES):
+            store(0, piece_nodes[q])
 
         for q in range(PIECES):
             y = products.tile([P, PIECE], F32, name="y")
             for kb in range(K_BLOCKS):
                 look_up(y, 1, q, kb)
-            finish(y, 1, q)
+            pooled = ring.tile([P, PIECE_NODES], F32, name="pooled")
+            pool_piece(pooled[:], y)
+            bias_and_relu(1, piece_nodes[q], pooled[:])
+            store(1, piece_nodes[q])

@@ -8,10 +8,10 @@ K, S = 256, 512
 M = 256
 N, D = 1024, 4
 PIECE = 256
+BANK = 512
 K_BLOCKS = K // P
 M_BLOCKS = M // P
 PIECES = N // PIECE
-PIECE_COLS = PIECE // 16
 PIECE_NODES = PIECE // D
 
 FLOPS = 2 * K * M * N
@@ -22,7 +22,7 @@ def tile_gather_matmul_kernel(tc, table, w, b, offs, out):
     with (
         tc.tile_pool(name="held", bufs=1) as held,
         tc.tile_pool(name="ring", bufs=2) as ring,
-        tc.psum_pool(name="products", bufs=PIECES) as products,
+        tc.psum_pool(name="products", bufs=4) as products,
     ):
         offsets = held.tile([P, N // 16], U16, name="offsets")
         windows = [held.tile([P, S], BF16, name="window%d" % kb) for kb in range(K_BLOCKS)]
@@ -43,13 +43,13 @@ def tile_gather_matmul_kernel(tc, table, w, b, offs, out):
         load_weights(nc.sync, 1, 0)
         load_weights(nc.scalar, 1, 1)
 
-        def look_up(y, mb, q, kb):
+        def look_up(y, mb, kb, first, entries, start, stop):
             nc.tensor.matmul(
-                y[:],
+                y,
                 weights[mb][kb][:],
-                windows[kb][:].indirect(offsets[:, q * PIECE_COLS : (q + 1) * PIECE_COLS]),
-                start=(kb == 0),
-                stop=(kb == K_BLOCKS - 1),
+                windows[kb][:].indirect(offsets[:, first // 16 : (first + entries) // 16]),
+                start=start,
+                stop=stop,
             )
 
         def pool_piece(pooled, y):
@@ -64,13 +64,24 @@ def tile_gather_matmul_kernel(tc, table, w, b, offs, out):
         piece_nodes = [slice(q * PIECE_NODES, (q + 1) * PIECE_NODES) for q in range(PIECES)]
         results = [held.tile([P, N // D], F32, name="result%d" % mb) for mb in range(M_BLOCKS)]
 
-        first_sums = [products.tile([P, PIECE], F32, name="y") for q in range(PIECES)]
-        for kb in range(K_BLOCKS):
-            for q in range(PIECES):
-                look_up(first_sums[q], 0, q, kb)
+        wide_sums = [products.tile([P, BANK], F32, name="y") for u in range(N // BANK)]
+        for u in range(N // BANK):
+            look_up(wide_sums[u][:], 0, 0, u * BANK, BANK, True, False)
+        steps = BANK // PIECE
+        for u in range(N // BANK):
+            for step in range(steps):
+                look_up(
+                    wide_sums[u][:, step * PIECE : (step + 1) * PIECE],
+                    0,
+                    1,
+                    u * BANK + step * PIECE,
+                    PIECE,
+                    False,
+                    step == steps - 1,
+                )
         pooled_block = held.tile([P, N // D], F32, name="pooled_block")
-        for q in range(PIECES):
-            pool_piece(pooled_block[:, piece_nodes[q]], first_sums[q])
+        for u in range(N // BANK):
+            pool_piece(pooled_block[:, u * (BANK // D) : (u + 1) * (BANK // D)], wide_sums[u])
         bias_and_relu(0, slice(0, N // D), pooled_block[:])
         for q in range(PIECES):
             store(0, piece_nodes[q])
@@ -78,7 +89,7 @@ def tile_gather_matmul_kernel(tc, table, w, b, offs, out):
         for q in range(PIECES):
             y = products.tile([P, PIECE], F32, name="y")
             for kb in range(K_BLOCKS):
-                look_up(y, 1, q, kb)
+                look_up(y[:], 1, kb, q * PIECE, PIECE, kb == 0, kb == K_BLOCKS - 1)
             pooled = ring.tile([P, PIECE_NODES], F32, name="pooled")
             pool_piece(pooled[:], y)
             bias_and_relu(1, piece_nodes[q], pooled[:])

@@ -87,10 +87,13 @@ def tile_gather_matmul_kernel(tc, table, w, b, offs, out):
             store(0, piece_nodes[q])
 
         for q in range(PIECES):
-            y = products.tile([P, PIECE], F32, name="y")
-            for kb in range(K_BLOCKS):
-                look_up(y[:], 1, kb, q * PIECE, PIECE, kb == 0, kb == K_BLOCKS - 1)
+            parts = 2 if q == PIECES - 1 else 1
+            entries = PIECE // parts
             pooled = ring.tile([P, PIECE_NODES], F32, name="pooled")
-            pool_piece(pooled[:], y)
+            for part in range(parts):
+                y = products.tile([P, entries], F32, name="y")
+                for kb in range(K_BLOCKS):
+                    look_up(y[:], 1, kb, q * PIECE + part * entries, entries, kb == 0, kb == K_BLOCKS - 1)
+                pool_piece(pooled[:, part * (entries // D) : (part + 1) * (entries // D)], y)
             bias_and_relu(1, piece_nodes[q], pooled[:])
             store(1, piece_nodes[q])

@@ -2,6 +2,7 @@ import concourse.mybir as mybir
 
 BF16, F32, U16 = mybir.dt.bfloat16, mybir.dt.float32, mybir.dt.uint16
 ADD, MAX = mybir.AluOpType.add, mybir.AluOpType.max
+RELU = mybir.ActivationFunctionType.Relu
 
 P = 128
 K, S = 256, 512
@@ -13,6 +14,7 @@ K_BLOCKS = K // P
 M_BLOCKS = M // P
 PIECES = N // PIECE
 PIECE_NODES = PIECE // D
+LAST_PARTS = (192, 64)
 
 FLOPS = 2 * K * M * N
 
@@ -21,7 +23,7 @@ def tile_gather_matmul_kernel(tc, table, w, b, offs, out):
     nc = tc.nc
     with (
         tc.tile_pool(name="held", bufs=1) as held,
-        tc.tile_pool(name="ring", bufs=2) as ring,
+        tc.tile_pool(name="ring", bufs=4) as ring,
         tc.psum_pool(name="products", bufs=4) as products,
     ):
         offsets = held.tile([P, N // 16], U16, name="offsets")
@@ -43,6 +45,11 @@ def tile_gather_matmul_kernel(tc, table, w, b, offs, out):
         load_weights(nc.sync, 1, 0)
         load_weights(nc.scalar, 1, 1)
 
+        zeros = held.tile([P, 1], F32, name="zeros")
+        nc.vector.memset(zeros[:], 0.0)
+        unused = held.tile([P, 1], F32, name="unused")
+        nc.scalar.activation(unused[:], zeros[:], RELU)
+
         def look_up(y, mb, kb, first, entries, start, stop):
             nc.tensor.matmul(
                 y,
@@ -55,8 +62,11 @@ def tile_gather_matmul_kernel(tc, table, w, b, offs, out):
         def pool_piece(pooled, y):
             nc.vector.tensor_reduce(pooled, y[:].rearrange("p (v d) -> p v d", d=D), axis=mybir.AxisListType.X, op=MAX)
 
-        def bias_and_relu(mb, nodes, pooled):
-            nc.vector.tensor_scalar(results[mb][:, nodes], pooled, bias[:, mb : mb + 1], 0.0, op0=ADD, op1=MAX)
+        def bias_and_relu(mb, nodes, pooled, last):
+            if last:
+                nc.vector.tensor_scalar(results[mb][:, nodes], pooled, bias[:, mb : mb + 1], 0.0, op0=ADD, op1=MAX)
+            else:
+                nc.scalar.activation(results[mb][:, nodes], pooled, RELU, bias=bias[:, mb : mb + 1])
 
         def store(mb, nodes):
             nc.sync.dma_start(out[mb * P : (mb + 1) * P, nodes], results[mb][:, nodes])
@@ -82,18 +92,18 @@ def tile_gather_matmul_kernel(tc, table, w, b, offs, out):
         pooled_block = held.tile([P, N // D], F32, name="pooled_block")
         for u in range(N // BANK):
             pool_piece(pooled_block[:, u * (BANK // D) : (u + 1) * (BANK // D)], wide_sums[u])
-        bias_and_relu(0, slice(0, N // D), pooled_block[:])
+        bias_and_relu(0, slice(0, N // D), pooled_block[:], False)
         for q in range(PIECES):
             store(0, piece_nodes[q])
 
         for q in range(PIECES):
-            parts = 2 if q == PIECES - 1 else 1
-            entries = PIECE // parts
             pooled = ring.tile([P, PIECE_NODES], F32, name="pooled")
-            for part in range(parts):
+            done = 0
+            for entries in LAST_PARTS if q == PIECES - 1 else (PIECE,):
                 y = products.tile([P, entries], F32, name="y")
                 for kb in range(K_BLOCKS):
-                    look_up(y[:], 1, kb, q * PIECE + part * entries, entries, kb == 0, kb == K_BLOCKS - 1)
-                pool_piece(pooled[:, part * (entries // D) : (part + 1) * (entries // D)], y)
-            bias_and_relu(1, piece_nodes[q], pooled[:])
+                    look_up(y[:], 1, kb, q * PIECE + done, entries, kb == 0, kb == K_BLOCKS - 1)
+                pool_piece(pooled[:, done // D : (done + entries) // D], y)
+                done += entries
+            bias_and_relu(1, piece_nodes[q], pooled[:], q == PIECES - 1)
             store(1, piece_nodes[q])

@@ -14,7 +14,7 @@ K_BLOCKS = K // P
 M_BLOCKS = M // P
 PIECES = N // PIECE
 PIECE_NODES = PIECE // D
-LAST_PARTS = (192, 64)
+LAST_PARTS = (160, 96)
 
 FLOPS = 2 * K * M * N
 
@@ -36,9 +36,9 @@ def tile_gather_matmul_kernel(tc, table, w, b, offs, out):
         def load_weights(queue, mb, kb):
             queue.dma_start(weights[mb][kb][:], w[kb * P : (kb + 1) * P, mb * P : (mb + 1) * P])
 
+        nc.sync.dma_start(windows[0][:], table[0:P, :])
+        load_weights(nc.scalar, 0, 0)
         nc.sync.dma_start(offsets[:], offs)
-        nc.scalar.dma_start(windows[0][:], table[0:P, :])
-        load_weights(nc.sync, 0, 0)
         load_weights(nc.scalar, 0, 1)
         nc.sync.dma_start(windows[1][:], table[P : 2 * P, :])
         nc.scalar.dma_start(bias[:], b.rearrange("(mb p) o -> p (mb o)", p=P))
@@ -62,8 +62,8 @@ def tile_gather_matmul_kernel(tc, table, w, b, offs, out):
         def pool_piece(pooled, y):
             nc.vector.tensor_reduce(pooled, y[:].rearrange("p (v d) -> p v d", d=D), axis=mybir.AxisListType.X, op=MAX)
 
-        def bias_and_relu(mb, nodes, pooled, last):
-            if last:
+        def bias_and_relu(mb, nodes, pooled, on_vector):
+            if on_vector:
                 nc.vector.tensor_scalar(results[mb][:, nodes], pooled, bias[:, mb : mb + 1], 0.0, op0=ADD, op1=MAX)
             else:
                 nc.scalar.activation(results[mb][:, nodes], pooled, RELU, bias=bias[:, mb : mb + 1])
@@ -105,5 +105,5 @@ def tile_gather_matmul_kernel(tc, table, w, b, offs, out):
                     look_up(y[:], 1, kb, q * PIECE + done, entries, kb == 0, kb == K_BLOCKS - 1)
                 pool_piece(pooled[:, done // D : (done + entries) // D], y)
                 done += entries
-            bias_and_relu(1, piece_nodes[q], pooled[:], q == PIECES - 1)
+            bias_and_relu(1, piece_nodes[q], pooled[:], q >= PIECES - 2)
             store(1, piece_nodes[q])

@@ -2,7 +2,6 @@ import concourse.mybir as mybir
 
 BF16, F32, U16 = mybir.dt.bfloat16, mybir.dt.float32, mybir.dt.uint16
 ADD, MAX = mybir.AluOpType.add, mybir.AluOpType.max
-RELU = mybir.ActivationFunctionType.Relu
 
 P = 128
 K, S = 256, 512
@@ -45,11 +44,6 @@ def tile_gather_matmul_kernel(tc, table, w, b, offs, out):
         load_weights(nc.sync, 1, 0)
         load_weights(nc.scalar, 1, 1)
 
-        zeros = held.tile([P, 1], F32, name="zeros")
-        nc.vector.memset(zeros[:], 0.0)
-        unused = held.tile([P, 1], F32, name="unused")
-        nc.scalar.activation(unused[:], zeros[:], RELU)
-
         def look_up(y, mb, kb, first, entries, start, stop):
             nc.tensor.matmul(
                 y,
@@ -62,14 +56,11 @@ def tile_gather_matmul_kernel(tc, table, w, b, offs, out):
         def pool_piece(pooled, y):
             nc.vector.tensor_reduce(pooled, y[:].rearrange("p (v d) -> p v d", d=D), axis=mybir.AxisListType.X, op=MAX)
 
-        def bias_and_relu(mb, nodes, pooled, on_vector):
-            if on_vector:
-                nc.vector.tensor_scalar(results[mb][:, nodes], pooled, bias[:, mb : mb + 1], 0.0, op0=ADD, op1=MAX)
-            else:
-                nc.scalar.activation(results[mb][:, nodes], pooled, RELU, bias=bias[:, mb : mb + 1])
+        def bias_and_relu(mb, nodes, pooled):
+            nc.vector.tensor_scalar(results[mb][:, nodes], pooled, bias[:, mb : mb + 1], 0.0, op0=ADD, op1=MAX)
 
-        def store(mb, nodes):
-            nc.sync.dma_start(out[mb * P : (mb + 1) * P, nodes], results[mb][:, nodes])
+        def store(queue, mb, nodes):
+            queue.dma_start(out[mb * P : (mb + 1) * P, nodes], results[mb][:, nodes])
 
         piece_nodes = [slice(q * PIECE_NODES, (q + 1) * PIECE_NODES) for q in range(PIECES)]
         results = [held.tile([P, N // D], F32, name="result%d" % mb) for mb in range(M_BLOCKS)]
@@ -92,9 +83,9 @@ def tile_gather_matmul_kernel(tc, table, w, b, offs, out):
         pooled_block = held.tile([P, N // D], F32, name="pooled_block")
         for u in range(N // BANK):
             pool_piece(pooled_block[:, u * (BANK // D) : (u + 1) * (BANK // D)], wide_sums[u])
-        bias_and_relu(0, slice(0, N // D), pooled_block[:], False)
+        bias_and_relu(0, slice(0, N // D), pooled_block[:])
         for q in range(PIECES):
-            store(0, piece_nodes[q])
+            store(nc.sync, 0, piece_nodes[q])
 
         for q in range(PIECES):
             pooled = ring.tile([P, PIECE_NODES], F32, name="pooled")
@@ -105,5 +96,5 @@ def tile_gather_matmul_kernel(tc, table, w, b, offs, out):
                     look_up(y[:], 1, kb, q * PIECE + done, entries, kb == 0, kb == K_BLOCKS - 1)
                 pool_piece(pooled[:, done // D : (done + entries) // D], y)
                 done += entries
-            bias_and_relu(1, piece_nodes[q], pooled[:], q >= PIECES - 2)
-            store(1, piece_nodes[q])
+            bias_and_relu(1, piece_nodes[q], pooled[:])
+            store(nc.sync, 1, piece_nodes[q])

@@ -35,8 +35,8 @@ def tile_gather_matmul_kernel(tc, table, w, b, offs, out):
         def load_weights(queue, mb, kb):
             queue.dma_start(weights[mb][kb][:], w[kb * P : (kb + 1) * P, mb * P : (mb + 1) * P])
 
-        nc.sync.dma_start(windows[0][:], table[0:P, :])
-        load_weights(nc.scalar, 0, 0)
+        load_weights(nc.sync, 0, 0)
+        nc.scalar.dma_start(windows[0][:], table[0:P, :])
         nc.sync.dma_start(offsets[:], offs)
         load_weights(nc.scalar, 0, 1)
         nc.sync.dma_start(windows[1][:], table[P : 2 * P, :])

@@ -94,7 +94,8 @@ def tile_gather_matmul_kernel(tc, table, w, b, offs, out):
                 y = products.tile([P, entries], F32, name="y")
                 for kb in range(K_BLOCKS):
                     look_up(y[:], 1, kb, q * PIECE + done, entries, kb == 0, kb == K_BLOCKS - 1)
-                pool_piece(pooled[:, done // D : (done + entries) // D], y)
+                part = slice(done // D, (done + entries) // D)
+                pool_piece(pooled[:, part], y)
+                bias_and_relu(1, slice(q * PIECE_NODES + part.start, q * PIECE_NODES + part.stop), pooled[:, part])
                 done += entries
-            bias_and_relu(1, piece_nodes[q], pooled[:])
             store(nc.sync, 1, piece_nodes[q])

import concourse.mybir as mybir

BF16, F32, U16 = mybir.dt.bfloat16, mybir.dt.float32, mybir.dt.uint16
ADD, MAX = mybir.AluOpType.add, mybir.AluOpType.max

P = 128
K, S = 256, 512
M = 256
N, D = 1024, 4
PIECE = 256
BANK = 512
K_BLOCKS = K // P
M_BLOCKS = M // P
PIECES = N // PIECE
PIECE_NODES = PIECE // D
LAST_PARTS = (160, 96)

FLOPS = 2 * K * M * N


def tile_gather_matmul_kernel(tc, table, w, b, offs, out):
    nc = tc.nc
    with (
        tc.tile_pool(name="held", bufs=1) as held,
        tc.tile_pool(name="ring", bufs=4) as ring,
        tc.psum_pool(name="products", bufs=4) as products,
    ):
        offsets = held.tile([P, N // 16], U16, name="offsets")
        windows = [held.tile([P, S], BF16, name="window%d" % kb) for kb in range(K_BLOCKS)]
        weights = [
            [held.tile([P, P], BF16, name="weights%d_%d" % (mb, kb)) for kb in range(K_BLOCKS)] for mb in range(M_BLOCKS)
        ]
        bias = held.tile([P, M_BLOCKS], F32, name="bias")

        def load_weights(queue, mb, kb):
            queue.dma_start(weights[mb][kb][:], w[kb * P : (kb + 1) * P, mb * P : (mb + 1) * P])

        load_weights(nc.sync, 0, 0)
        nc.scalar.dma_start(windows[0][:], table[0:P, :])
        nc.sync.dma_start(offsets[:], offs)
        load_weights(nc.scalar, 0, 1)
        nc.sync.dma_start(windows[1][:], table[P : 2 * P, :])
        nc.scalar.dma_start(bias[:], b.rearrange("(mb p) o -> p (mb o)", p=P))
        load_weights(nc.sync, 1, 0)
        load_weights(nc.scalar, 1, 1)

        def look_up(y, mb, kb, first, entries, start, stop):
            nc.tensor.matmul(
                y,
                weights[mb][kb][:],
                windows[kb][:].indirect(offsets[:, first // 16 : (first + entries) // 16]),
                start=start,
                stop=stop,
            )

        def pool_piece(pooled, y):
            nc.vector.tensor_reduce(pooled, y[:].rearrange("p (v d) -> p v d", d=D), axis=mybir.AxisListType.X, op=MAX)

        def bias_and_relu(mb, nodes, pooled):
            nc.vector.tensor_scalar(results[mb][:, nodes], pooled, bias[:, mb : mb + 1], 0.0, op0=ADD, op1=MAX)

        def store(queue, mb, nodes):
            queue.dma_start(out[mb * P : (mb + 1) * P, nodes], results[mb][:, nodes])

        piece_nodes = [slice(q * PIECE_NODES, (q + 1) * PIECE_NODES) for q in range(PIECES)]
        results = [held.tile([P, N // D], F32, name="result%d" % mb) for mb in range(M_BLOCKS)]

        wide_sums = [products.tile([P, BANK], F32, name="y") for u in range(N // BANK)]
        for u in range(N // BANK):
            look_up(wide_sums[u][:], 0, 0, u * BANK, BANK, True, False)
        steps = BANK // PIECE
        for u in range(N // BANK):
            for step in range(steps):
                look_up(
                    wide_sums[u][:, step * PIECE : (step + 1) * PIECE],
                    0,
                    1,
                    u * BANK + step * PIECE,
                    PIECE,
                    False,
                    step == steps - 1,
                )
        pooled_block = held.tile([P, N // D], F32, name="pooled_block")
        for u in range(N // BANK):
            pool_piece(pooled_block[:, u * (BANK // D) : (u + 1) * (BANK // D)], wide_sums[u])
        bias_and_relu(0, slice(0, N // D), pooled_block[:])
        for q in range(PIECES):
            store(nc.sync, 0, piece_nodes[q])

        for q in range(PIECES):
            pooled = ring.tile([P, PIECE_NODES], F32, name="pooled")
            done = 0
            for entries in LAST_PARTS if q == PIECES - 1 else (PIECE,):
                y = products.tile([P, entries], F32, name="y")
                for kb in range(K_BLOCKS):
                    look_up(y[:], 1, kb, q * PIECE + done, entries, kb == 0, kb == K_BLOCKS - 1)
                part = slice(done // D, (done + entries) // D)
                pool_piece(pooled[:, part], y)
                bias_and_relu(1, slice(q * PIECE_NODES + part.start, q * PIECE_NODES + part.stop), pooled[:, part])
                done += entries
            store(nc.sync, 1, piece_nodes[q])
